import numpy as np
import ml_dtypes


def mxq(x, axis, fmt="e4m3"):
    dtype, down = {"e4m3": (ml_dtypes.float8_e4m3fn, 7), "e5m2": (ml_dtypes.float8_e5m2, 14)}[fmt]
    v = np.moveaxis(np.asarray(x, np.float32).astype(ml_dtypes.bfloat16).astype(np.float64), axis, -1)
    blocks = v.reshape(v.shape[:-1] + (-1, 32))
    amax = np.abs(blocks).max(-1, keepdims=True)
    byte = np.maximum(np.where(amax > 0, np.frexp(amax)[1] - 1 + 127, 0) - down, 1)
    scale = np.exp2(byte - 127.0)
    codes = (blocks / scale).astype(np.float32).astype(dtype).astype(np.float64)
    return np.moveaxis((codes * scale).reshape(v.shape), -1, axis)


WIDE = False


def mx_kscale(k):
    if not WIDE:
        return np.ones(k)
    levels = np.array([10, -10, 5, -5, 0])
    if k % 512:
        return np.exp2(np.random.permutation(np.resize(levels, k // 32))).repeat(32)
    a = np.empty((k // 512, 16))
    for p in range(k // 512):
        a[p, :8] = np.random.permutation(np.resize(levels, 8))
        for g in range(8):
            far = levels[np.abs(levels - a[p, g]) >= 10]
            a[p, g + 8] = far[np.random.randint(len(far))]
    return np.exp2(a.ravel()).repeat(32)


def f64(x):
    return np.asarray(x).astype(np.float64)


def striped(idx):
    return np.tile(idx.reshape(-1, 16).T, (8, 1)).astype(np.uint16)


def unstriped(offs):
    return offs[:16].T.reshape(-1).astype(np.int64)


E2M1 = np.array([0.0, 0.5, 1.0, 1.5, 2.0, 3.0, 4.0, 6.0, -0.0, -0.5, -1.0, -1.5, -2.0, -3.0, -4.0, -6.0])


def pack_weight(w, fmt):
    k, n = w.shape
    w = f64(np.asarray(w, np.float32).astype(ml_dtypes.bfloat16)).reshape(k // 32, 32, n)
    amax = np.abs(w).max(1)
    if fmt == "e4m3":
        byte = np.frexp(amax)[1] - 1 + 127 - 7
    else:
        mant, ex = np.frexp(amax / 6.0)
        byte = np.where(mant > 0.5, ex, ex - 1) + 127
    byte = np.clip(np.where(amax > 0, byte, 1), 1, 254)
    scaled = (w * np.exp2(127.0 - byte)[:, None, :]).reshape(k, n).astype(np.float32)
    by_word = np.ascontiguousarray(scaled.reshape(k // 512, 128, 4, n).transpose(0, 1, 3, 2))
    if fmt == "e4m3":
        words = by_word.astype(ml_dtypes.float8_e4m3fn).view(np.uint8)
    else:
        c = by_word.astype(ml_dtypes.float4_e2m1fn).view(np.uint8) & 0xF
        words = (c[..., 0::2] | (c[..., 1::2] << 4)).reshape(k // 512, 128, 2 * n)
    return np.ascontiguousarray(words), np.ascontiguousarray(byte.astype(np.uint8).reshape(k // 512, 16, n))


def unpack_weight(words, scales, fmt):
    g, _, n = scales.shape
    words = np.ascontiguousarray(words).reshape(g, 128, n, -1)
    if fmt == "e4m3":
        vals = words.view(ml_dtypes.float8_e4m3fn).astype(np.float64)
    else:
        nib = np.empty((g, 128, n, 4), np.uint8)
        nib[..., 0::2] = words & 0xF
        nib[..., 1::2] = words >> 4
        vals = E2M1[nib]
    vals = vals * np.repeat(np.exp2(scales.astype(np.float64) - 127.0), 8, axis=1)[..., None]
    return vals.transpose(0, 1, 3, 2).reshape(g * 512, n)


def silu(v):
    return v / (1.0 + np.exp(-np.maximum(v, -700.0)))


K, T, E, C, H, N = 1536, 512, 8, 128, 512, 256
TOP = 4
PAD = 64


def by_expert(wq, xq):
    return np.concatenate([wq[e].T @ xq[:, e * C:(e + 1) * C] for e in range(E)], axis=1)


def setup_inputs():
    n = np.random.standard_normal
    s = mx_kscale(K)[:, None]
    u = mx_kscale(H)
    slot_token = np.empty(E * C, np.int64); pos = np.tile(E * C + np.arange(T) % PAD, (TOP, 1)); taken = np.zeros(T, np.int64)
    liked = np.random.randn(T)
    for e in np.random.permutation(E):
        free = np.flatnonzero(taken < TOP); pick = np.random.permutation(free[np.argsort(-(liked[free] + np.random.gumbel(size=free.size)))[:C]]); slot_token[e * C:(e + 1) * C] = pick
        pos[taken[pick], pick] = e * C + np.arange(C); taken[pick] += 1
    g = np.random.uniform(0.2, 0.8, (TOP, T))
    w1 = [pack_weight(m, "e2m1") for m in n((E, K, H)) / np.sqrt(K) / s[None] * u[None, None, :]]
    w2 = [pack_weight(m, "e2m1") for m in n((E, H, N)) / np.sqrt(H) / u[None, :, None]]
    return {
        "xT": (n((K, T)) * s).astype(np.float32),
        "w1_words": np.stack([m[0] for m in w1]),
        "w1_scales": np.stack([m[1] for m in w1]),
        "w2_words": np.stack([m[0] for m in w2]),
        "w2_scales": np.stack([m[1] for m in w2]),
        "gate": np.stack([np.tile(r, (N, 1)) for r in g]).astype(np.float32),
        "offs": striped(slot_token),
        "pos1": striped(pos[0]),
        "pos2": striped(pos[1]),
        "pos3": striped(pos[2]),
        "pos4": striped(pos[3]),
    }


def reference(xT, w1_words, w1_scales, w2_words, w2_scales, gate, offs, pos1, pos2, pos3, pos4):
    idx = unstriped(offs)
    w1 = np.stack([unpack_weight(w1_words[e], w1_scales[e], "e2m1") for e in range(E)])
    w2 = np.stack([unpack_weight(w2_words[e], w2_scales[e], "e2m1") for e in range(E)])
    xq = mxq(f64(xT)[:, idx], 0, "e4m3")
    h = silu(by_expert(w1, xq))
    y = by_expert(w2, mxq(h, 0, "e4m3"))
    y = np.concatenate([y, np.zeros((N, PAD))], axis=1)
    return sum(f64(gate[r]) * y[:, unstriped(p)] for r, p in enumerate((pos1, pos2, pos3, pos4)))

@@ -1,0 +1,259 @@
+from contextlib import ExitStack
+
+import concourse.mybir as mybir
+from concourse.masks import make_identity
+
+K, T, E, C, H, N = 1536, 512, 8, 128, 512, 256
+TOP, PAD = 4, 64
+S = E * C
+FLOPS = 2 * S * (K * H + H * N)
+
+F32 = mybir.dt.float32
+BF16 = mybir.dt.bfloat16
+I32 = mybir.dt.int32
+U32 = mybir.dt.uint32
+U16 = mybir.dt.uint16
+U8 = mybir.dt.uint8
+FP8X4 = mybir.dt.float8_e4m3fn_x4
+FP4X4 = mybir.dt.float4_e2m1fn_x4
+COPY = mybir.ActivationFunctionType.Copy
+SILU = mybir.ActivationFunctionType.Silu
+MULT = mybir.AluOpType.mult
+ADD = mybir.AluOpType.add
+
+P = 128
+PACK = 4
+K_PASS = P * PACK
+PASSES = K // K_PASS
+HALVES = N // P
+PAIR = 2 * C
+VEC_TOKENS = 160
+W2_GROUP = 4
+
+
+def tile_moe_ecr_mlp_silu_kernel(
+    tc, xT, w1_words, w1_scales, w2_words, w2_scales, gate, offs, pos1, pos2, pos3, pos4, out
+):
+    nc = tc.nc
+    with ExitStack() as ctx:
+        keep = ctx.enter_context(tc.tile_pool(name="keep", bufs=1))
+        ring = ctx.enter_context(tc.tile_pool(name="ring", bufs=3))
+        psum = ctx.enter_context(tc.psum_pool(name="psum", bufs=1))
+
+        w1_sc = [keep.tile([P, W2_GROUP * PASSES * H], U8, name="w1_sc%d" % g, align_bytes=64) for g in range(E // W2_GROUP)]
+        w2_sc = keep.tile([P, E * N], U8, name="w2_sc", align_bytes=64)
+        x_sc0 = keep.tile([P, T], U8, name="x_sc0", align_bytes=64)
+        x_sc12 = keep.tile([P, 2 * T], U8, name="x_sc12", align_bytes=64)
+        zeros = keep.tile([P, PAD], F32, name="zeros")
+        nc.vector.memset(zeros[:], 0.0)
+        nc.vector.memset(w1_sc[0][:].bitcast(I32), 0)
+        for plane in (x_sc0, x_sc12, w1_sc[1], w2_sc):
+            nc.gpsimd.memset(plane[:].bitcast(I32), 0)
+        ident = keep.tile([P, P], F32, name="ident")
+        make_identity(nc, ident[:])
+
+        y = [keep.tile([P, S + PAD], F32, name="y%d" % hf) for hf in range(HALVES)]
+        for hf in range(HALVES):
+            nc.scalar.activation(y[hf][:, S:], zeros[:], SILU)
+
+        x_first = [keep.tile([P, PACK, T // 2], F32, name="x_first%d" % i) for i in range(2)]
+        x_raw = {s: keep.tile([P, PACK, T], F32, name="x_raw%d" % s) for s in range(1, PASSES)}
+        offs_t = keep.tile([P, S // 16], U16, name="offs_t")
+        pos_t = [keep.tile([P, T // 16], U16, name="pos_t%d" % r) for r in range(TOP)]
+        w2_w = keep.tile([P, E, 2 * N], U8, name="w2_w", align_bytes=64)
+        gate_t = keep.tile([P, TOP, T], F32, name="gate_t")
+        w1_w = {}
+
+        def load_tokens(s):
+            rows = xT[s * K_PASS:(s + 1) * K_PASS, :].rearrange("(p j) t -> p j t", j=PACK)
+            for j in (0, 2):
+                nc.sync.dma_start(x_raw[s][:, j:j + 2, :], rows[:, j:j + 2, :])
+
+        def load_scale_rows(plane, scales):
+            rows = scales.rearrange("e s (q r) i -> r q (e s) i", r=4)
+            for r in range(4):
+                nc.sync.dma_start(
+                    plane[r:P:32, :].bitcast(I32).rearrange("q (g i) -> q g i", g=rows.shape[2]), rows[r].bitcast(I32)
+                )
+
+        def load_w1(e0, e1):
+            words = keep.tile([P, (e1 - e0) * PASSES, 2 * H], U8, name="w1_w%d" % e0, align_bytes=64)
+            nc.sync.dma_start(words[:].bitcast(I32), w1_words[e0:e1].rearrange("e s p b -> p (e s) b").bitcast(I32))
+            for e in range(e0, e1):
+                w1_w[e] = (words, (e - e0) * PASSES)
+
+        first_rows = xT[0:K_PASS, :].rearrange("(p j) t -> p j t", j=PACK)
+        for i in range(2):
+            nc.sync.dma_start(x_first[i][:], first_rows[:, :, i * T // 2:(i + 1) * T // 2])
+        nc.sync.dma_start(offs_t[:], offs)
+        load_tokens(1)
+        load_tokens(2)
+        nc.sync.dma_start(pos_t[0][:], pos1)
+        load_scale_rows(w1_sc[0], w1_scales[0:W2_GROUP])
+        load_w1(0, 2)
+        load_scale_rows(w1_sc[1], w1_scales[W2_GROUP:E])
+        load_w1(2, 4)
+        load_w1(4, 6)
+        load_w1(6, 7)
+        load_w1(7, 8)
+        load_scale_rows(w2_sc, w2_scales)
+        nc.sync.dma_start(w2_w[:].bitcast(I32), w2_words.rearrange("e s p b -> p (e s) b").bitcast(I32))
+        for r, pos in ((1, pos2), (2, pos3), (3, pos4)):
+            nc.sync.dma_start(pos_t[r][:], pos)
+        for r in (2, 0):
+            nc.sync.dma_start(gate_t[:, r:r + 2, :], gate[r:r + 2, 0:P, :].rearrange("r p t -> p r t"))
+
+        x_bf = [keep.tile([P, T, PACK], BF16, name="x_bf%d" % s, align_bytes=64) for s in range(PASSES)]
+        x_w0 = keep.tile([P, T], U32, name="x_w0", align_bytes=64)
+        x_w12 = keep.tile([P, 2 * T], U32, name="x_w12", align_bytes=64)
+        x_w = [x_w0[:], x_w12[:, 0:T], x_w12[:, T:2 * T]]
+        x_sc = [x_sc0[:], x_sc12[:, 0:T], x_sc12[:, T:2 * T]]
+
+        def cast(engine, s, raw, t0):
+            dst = x_bf[s][:, t0:t0 + raw.shape[2], :].rearrange("p (c i) j -> p c j i", i=4)
+            src = raw.rearrange("p j (c i) -> p c j i", i=4)
+            if engine == "vector":
+                nc.vector.tensor_copy(dst, src)
+            else:
+                nc.scalar.activation(dst, src, COPY)
+
+        def quantise_tokens(s, t0, t1):
+            nc.vector.quantize_mx(
+                out=x_w[s][:, t0:t1].bitcast(FP8X4),
+                scales=x_sc[s][:, t0:t1],
+                in_=x_bf[s][:, t0:t1, :].rearrange("p t j -> p (t j)"),
+            )
+
+        g_w = [keep.tile([P, S], U32, name="g_w%d" % s, align_bytes=64) for s in range(PASSES)]
+        g_sc = [keep.tile([P, S], U8, name="g_sc%d" % s, align_bytes=64) for s in range(PASSES)]
+
+        def gather(dst, window, e0, e1):
+            nc.vector.tensor_copy(dst[:, e0 * C:e1 * C], window.indirect(offs_t[:, e0 * C // 16:e1 * C // 16]))
+
+        bank = [psum.tile([P, H], F32, name="bank%d" % e) for e in range(E)]
+
+        def first_product(s, e, start, stop):
+            slots = slice(e * C, (e + 1) * C)
+            words, row = w1_w[e]
+            g = (e % W2_GROUP) * PASSES + s
+            nc.tensor.matmul_mx(
+                out=bank[e][:],
+                lhsT=g_w[s][:, slots].bitcast(FP8X4),
+                lhsT_scale=g_sc[s][:, slots],
+                rhs=words[:, row + s, :].bitcast(FP4X4),
+                rhs_scale=w1_sc[e // W2_GROUP][:, g * H:(g + 1) * H],
+                start=start,
+                stop=stop,
+            )
+
+        def first_products(e0, e1):
+            for s in range(PASSES):
+                for e in range(e0, e1):
+                    first_product(s, e, s == 0, s == PASSES - 1)
+
+        h_bf = {}
+
+        def hidden(e):
+            h_t = ring.tile([P, H], BF16, name="h_t", align_bytes=64)
+            nc.scalar.activation(
+                h_t[:].rearrange("c (u p d) -> c u p d", u=2, d=2),
+                bank[e][:].rearrange("c (p u d) -> c u p d", u=2, d=2),
+                SILU,
+            )
+            words = h_t[:].bitcast(F32)
+            for u in range(2):
+                nc.tensor.transpose(bank[e][:, u * C:(u + 1) * C], words[:, u * P:(u + 1) * P], ident[:])
+            h_bf[e] = keep.tile([P, C * PACK], BF16, name="h_bf%d" % e, align_bytes=64)
+            nc.scalar.copy(
+                h_bf[e][:].bitcast(F32).rearrange("p (c u) -> p c u", u=2),
+                bank[e][:, 0:2 * C].rearrange("p (u c) -> p c u", u=2),
+            )
+
+        h_w = keep.tile([P, S], U32, name="h_w", align_bytes=64)
+        h_sc = keep.tile([P, S], U8, name="h_sc", align_bytes=64)
+
+        def quantise_hidden(e):
+            slots = slice(e * C, (e + 1) * C)
+            nc.vector.quantize_mx(out=h_w[:, slots].bitcast(FP8X4), scales=h_sc[:, slots], in_=h_bf[e][:])
+
+        def second_products(hf, e0, e1, bank_no, copy):
+            acc = psum.tile([P, H], F32, name="y%d_%d" % (hf, e0), tag="bank%d" % bank_no)
+            for e in range(e0, e1):
+                slots = slice(e * C, (e + 1) * C)
+                nc.tensor.matmul_mx(
+                    out=acc[:, (e - e0) * C:(e - e0 + 1) * C],
+                    lhsT=w2_w[:, e, hf * 2 * P:(hf + 1) * 2 * P].bitcast(FP4X4),
+                    lhsT_scale=w2_sc[:, e * N + hf * P:e * N + (hf + 1) * P],
+                    rhs=h_w[:, slots].bitcast(FP8X4),
+                    rhs_scale=h_sc[:, slots],
+                    start=True,
+                    stop=True,
+                )
+            copy(y[hf][:, e0 * C:e1 * C], acc[:, 0:(e1 - e0) * C])
+
+        STEPS = ((0, 2), (2, 4), (4, 6), (6, 7), (7, 8))
+        half = T // 2
+        cast("vector", 0, x_first[0][:], 0)
+        quantise_tokens(0, 0, half)
+        cast("vector", 0, x_first[1][:, :, 0:VEC_TOKENS], half)
+        cast("scalar", 0, x_first[1][:, :, VEC_TOKENS:half], half + VEC_TOKENS)
+        quantise_tokens(0, half, T)
+        for e0 in range(0, E, 2):
+            gather(g_w[0], x_w[0], e0, e0 + 2)
+            gather(g_sc[0], x_sc[0], e0, e0 + 2)
+        cast("scalar", 1, x_raw[1][:], 0)
+        quantise_tokens(1, 0, T)
+        gather(g_w[1], x_w[1], 0, 2)
+        gather(g_sc[1], x_sc[1], 0, 2)
+        cast("scalar", 2, x_raw[2][:], 0)
+        quantise_tokens(2, 0, T)
+        for e0, e1 in STEPS:
+            if e0 > 0:
+                gather(g_w[1], x_w12[:], e0, e1)
+                gather(g_sc[1], x_sc12[:], e0, e1)
+            gather(g_w[2], x_w[2], e0, e1)
+            gather(g_sc[2], x_sc[2], e0, e1)
+        for step, (e0, e1) in enumerate(STEPS):
+            first_products(e0, e1)
+            if step > 0:
+                for e in range(*STEPS[step - 1]):
+                    hidden(e)
+                    quantise_hidden(e)
+        hidden(E - 1)
+        quantise_hidden(E - 1)
+        second_products(0, 4, 6, 6, nc.vector.tensor_copy)
+        second_products(0, 6, 7, 0, nc.vector.tensor_copy)
+        second_products(0, 0, 4, 7, nc.scalar.copy)
+        second_products(0, 7, 8, 1, nc.vector.tensor_copy)
+        second_products(1, 0, 4, 1, nc.scalar.copy)
+        second_products(1, 4, 8, 7, nc.scalar.copy)
+
+        prod = {}
+
+        def weighted(hf, r):
+            prod[hf, r] = keep.tile([P, T], F32, name="prod%d_%d" % (hf, r))
+            nc.vector.tensor_tensor(prod[hf, r][:], y[hf][:].indirect(pos_t[r][:]), gate_t[:, r, :], MULT)
+
+        back = {}
+        SUM_BANKS = ((2, 3, 4, 5), (0, 6, 1, 7))
+        chunks = T // P
+        for hf in range(HALVES):
+            sums = [psum.tile([P, H], F32, name="sums%d_%d" % (hf, c), tag="bank%d" % SUM_BANKS[hf][c]) for c in range(chunks)]
+            for r in range(TOP - 1, 0, -1):
+                weighted(hf, r)
+                for c in range(chunks):
+                    nc.tensor.matmul(
+                        sums[c][:, 0:P], prod[hf, r][:, c * P:(c + 1) * P], ident[:],
+                        start=(r == TOP - 1), stop=(r == 1), is_transpose=True,
+                    )
+            turned = keep.tile([P, T], F32, name="turned%d" % hf)
+            for c in range(chunks):
+                nc.scalar.copy(turned[:, c * P:(c + 1) * P], sums[c][:, 0:P])
+            back[hf] = psum.tile([P, H], F32, name="back%d" % hf, tag="bank%d" % SUM_BANKS[hf][0])
+            for c in range(chunks):
+                nc.tensor.transpose(back[hf][:, c * P:(c + 1) * P], turned[:, c * P:(c + 1) * P], ident[:])
+        for hf in range(HALVES):
+            weighted(hf, 0)
+            total = keep.tile([P, T], F32, name="total%d" % hf)
+            nc.vector.tensor_tensor(total[:], back[hf][:], prod[hf, 0][:], ADD)
+            nc.sync.dma_start(out[hf * P:(hf + 1) * P, :], total[:])

@@ -29,6 +29,7 @@ HALVES = N // P
 PAIR = 2 * C
 VEC_TOKENS = 160
 W2_GROUP = 4
+SPARE = 192
 
 
 def tile_moe_ecr_mlp_silu_kernel(
@@ -42,13 +43,15 @@ def tile_moe_ecr_mlp_silu_kernel(
 
         w1_sc = [keep.tile([P, W2_GROUP * PASSES * H], U8, name="w1_sc%d" % g, align_bytes=64) for g in range(E // W2_GROUP)]
         w2_sc = keep.tile([P, E * N], U8, name="w2_sc", align_bytes=64)
-        x_sc0 = keep.tile([P, T], U8, name="x_sc0", align_bytes=64)
+        x_sc0 = keep.tile([P, T + SPARE], U8, name="x_sc0", align_bytes=64)
+        x_w0 = keep.tile([P, T + SPARE], I32, name="x_w0", align_bytes=64)
         x_sc12 = keep.tile([P, 2 * T], U8, name="x_sc12", align_bytes=64)
         zeros = keep.tile([P, PAD], F32, name="zeros")
         nc.vector.memset(zeros[:], 0.0)
-        nc.vector.memset(w1_sc[0][:].bitcast(I32), 0)
-        for plane in (x_sc0, x_sc12, w1_sc[1], w2_sc):
-            nc.gpsimd.memset(plane[:].bitcast(I32), 0)
+        nc.vector.memset(x_w0[:, T:], 0)
+        for plane in (x_sc0, w1_sc[0], x_sc12, w1_sc[1]):
+            nc.vector.memset(plane[:].bitcast(I32), 0)
+        nc.gpsimd.memset(w2_sc[:].bitcast(I32), 0)
         ident = keep.tile([P, P], F32, name="ident")
         make_identity(nc, ident[:])
 
@@ -91,11 +94,10 @@ def tile_moe_ecr_mlp_silu_kernel(
         nc.sync.dma_start(pos_t[0][:], pos1)
         load_scale_rows(w1_sc[0], w1_scales[0:W2_GROUP])
         load_w1(0, 2)
-        load_scale_rows(w1_sc[1], w1_scales[W2_GROUP:E])
         load_w1(2, 4)
+        load_scale_rows(w1_sc[1], w1_scales[W2_GROUP:E])
         load_w1(4, 6)
-        load_w1(6, 7)
-        load_w1(7, 8)
+        load_w1(6, 8)
         load_scale_rows(w2_sc, w2_scales)
         nc.sync.dma_start(w2_w[:].bitcast(I32), w2_words.rearrange("e s p b -> p (e s) b").bitcast(I32))
         for r, pos in ((1, pos2), (2, pos3), (3, pos4)):
@@ -104,10 +106,9 @@ def tile_moe_ecr_mlp_silu_kernel(
             nc.sync.dma_start(gate_t[:, r:r + 2, :], gate[r:r + 2, 0:P, :].rearrange("r p t -> p r t"))
 
         x_bf = [keep.tile([P, T, PACK], BF16, name="x_bf%d" % s, align_bytes=64) for s in range(PASSES)]
-        x_w0 = keep.tile([P, T], U32, name="x_w0", align_bytes=64)
         x_w12 = keep.tile([P, 2 * T], U32, name="x_w12", align_bytes=64)
-        x_w = [x_w0[:], x_w12[:, 0:T], x_w12[:, T:2 * T]]
-        x_sc = [x_sc0[:], x_sc12[:, 0:T], x_sc12[:, T:2 * T]]
+        x_w = [x_w0[:, 0:T].bitcast(U32), x_w12[:, 0:T], x_w12[:, T:2 * T]]
+        x_sc = [x_sc0[:, 0:T], x_sc12[:, 0:T], x_sc12[:, T:2 * T]]
 
         def cast(engine, s, raw, t0):
             dst = x_bf[s][:, t0:t0 + raw.shape[2], :].rearrange("p (c i) j -> p c j i", i=4)
@@ -164,7 +165,8 @@ def tile_moe_ecr_mlp_silu_kernel(
             for u in range(2):
                 nc.tensor.transpose(bank[e][:, u * C:(u + 1) * C], words[:, u * P:(u + 1) * P], ident[:])
             h_bf[e] = keep.tile([P, C * PACK], BF16, name="h_bf%d" % e, align_bytes=64)
-            nc.scalar.copy(
+            copy = nc.vector.tensor_copy if e in (E - 4, E - 3) else nc.scalar.copy
+            copy(
                 h_bf[e][:].bitcast(F32).rearrange("p (c u) -> p c u", u=2),
                 bank[e][:, 0:2 * C].rearrange("p (u c) -> p c u", u=2),
             )
@@ -198,9 +200,9 @@ def tile_moe_ecr_mlp_silu_kernel(
         cast("vector", 0, x_first[1][:, :, 0:VEC_TOKENS], half)
         cast("scalar", 0, x_first[1][:, :, VEC_TOKENS:half], half + VEC_TOKENS)
         quantise_tokens(0, half, T)
-        for e0 in range(0, E, 2):
-            gather(g_w[0], x_w[0], e0, e0 + 2)
-            gather(g_sc[0], x_sc[0], e0, e0 + 2)
+        for e0 in range(0, E, 4):
+            gather(g_w[0], x_w0[:].bitcast(U32), e0, e0 + 4)
+            gather(g_sc[0], x_sc0[:], e0, e0 + 4)
         cast("scalar", 1, x_raw[1][:], 0)
         quantise_tokens(1, 0, T)
         gather(g_w[1], x_w[1], 0, 2)
@@ -208,22 +210,23 @@ def tile_moe_ecr_mlp_silu_kernel(
         cast("scalar", 2, x_raw[2][:], 0)
         quantise_tokens(2, 0, T)
         for e0, e1 in STEPS:
-            if e0 > 0:
-                gather(g_w[1], x_w12[:], e0, e1)
-                gather(g_sc[1], x_sc12[:], e0, e1)
+            if e0 > 0 and e0 % 2 == 0:
+                gather(g_w[1], x_w12[:], e0, e0 + 2)
+                gather(g_sc[1], x_sc12[:], e0, e0 + 2)
             gather(g_w[2], x_w[2], e0, e1)
             gather(g_sc[2], x_sc[2], e0, e1)
-        for step, (e0, e1) in enumerate(STEPS):
-            first_products(e0, e1)
-            if step > 0:
-                for e in range(*STEPS[step - 1]):
-                    hidden(e)
-                    quantise_hidden(e)
-        hidden(E - 1)
-        quantise_hidden(E - 1)
-        second_products(0, 4, 6, 6, nc.vector.tensor_copy)
+        for e0 in range(0, E, 2):
+            first_products(e0, e0 + 2)
+            for e in range(max(e0 - 2, 0), e0):
+                hidden(e)
+                quantise_hidden(e)
+        for e in (E - 2, E - 1):
+            hidden(e)
+        for e in (E - 2, E - 1):
+            quantise_hidden(e)
+        second_products(0, 0, 4, 6, nc.scalar.copy)
         second_products(0, 6, 7, 0, nc.vector.tensor_copy)
-        second_products(0, 0, 4, 7, nc.scalar.copy)
+        second_products(0, 4, 6, 7, nc.scalar.copy)
         second_products(0, 7, 8, 1, nc.vector.tensor_copy)
         second_products(1, 0, 4, 1, nc.scalar.copy)
         second_products(1, 4, 8, 7, nc.scalar.copy)
@@ -252,8 +255,11 @@ def tile_moe_ecr_mlp_silu_kernel(
             back[hf] = psum.tile([P, H], F32, name="back%d" % hf, tag="bank%d" % SUM_BANKS[hf][0])
             for c in range(chunks):
                 nc.tensor.transpose(back[hf][:, c * P:(c + 1) * P], turned[:, c * P:(c + 1) * P], ident[:])
-        for hf in range(HALVES):
-            weighted(hf, 0)
-            total = keep.tile([P, T], F32, name="total%d" % hf)
-            nc.vector.tensor_tensor(total[:], back[hf][:], prod[hf, 0][:], ADD)
-            nc.sync.dma_start(out[hf * P:(hf + 1) * P, :], total[:])
+        for hf, t0, t1 in ((0, 0, T), (1, 0, T // 2), (1, T // 2, T)):
+            last = keep.tile([P, t1 - t0], F32, name="last%d_%d" % (hf, t0))
+            nc.vector.tensor_tensor(
+                last[:], y[hf][:].indirect(pos_t[0][:, t0 // 16:t1 // 16]), gate_t[:, 0, t0:t1], MULT
+            )
+            total = keep.tile([P, t1 - t0], F32, name="total%d_%d" % (hf, t0))
+            nc.vector.tensor_tensor(total[:], back[hf][:, t0:t1], last[:], ADD)
+            nc.sync.dma_start(out[hf * P:(hf + 1) * P, t0:t1], total[:])

@@ -64,7 +64,7 @@ def tile_moe_ecr_mlp_silu_kernel(
         offs_t = keep.tile([P, S // 16], U16, name="offs_t")
         pos_t = [keep.tile([P, T // 16], U16, name="pos_t%d" % r) for r in range(TOP)]
         w2_w = keep.tile([P, E, 2 * N], U8, name="w2_w", align_bytes=64)
-        gate_t = keep.tile([P, TOP, T], F32, name="gate_t")
+        gate_t = [keep.tile([P, T], F32, name="gate_t%d" % r) for r in range(TOP)]
         w1_w = {}
 
         def load_tokens(s):
@@ -79,11 +79,18 @@ def tile_moe_ecr_mlp_silu_kernel(
                     plane[r:P:32, :].bitcast(I32).rearrange("q (g i) -> q g i", g=rows.shape[2]), rows[r].bitcast(I32)
                 )
 
-        def load_w1(e0, e1):
-            words = keep.tile([P, (e1 - e0) * PASSES, 2 * H], U8, name="w1_w%d" % e0, align_bytes=64)
-            nc.sync.dma_start(words[:].bitcast(I32), w1_words[e0:e1].rearrange("e s p b -> p (e s) b").bitcast(I32))
-            for e in range(e0, e1):
-                w1_w[e] = (words, (e - e0) * PASSES)
+        def load_w1_first(e0):
+            words = keep.tile([P, W2_GROUP, 2 * H], U8, name="w1_first%d" % e0, align_bytes=64)
+            src = w1_words[e0:e0 + W2_GROUP, 0].rearrange("e p b -> p e b")
+            nc.sync.dma_start(words[:].bitcast(I32), src.bitcast(I32))
+            for e in range(e0, e0 + W2_GROUP):
+                w1_w[e, 0] = words[:, e - e0, :]
+
+        def load_w1_rest(e):
+            words = keep.tile([P, PASSES - 1, 2 * H], U8, name="w1_rest%d" % e, align_bytes=64)
+            nc.sync.dma_start(words[:].bitcast(I32), w1_words[e, 1:PASSES].rearrange("s p b -> p s b").bitcast(I32))
+            for s in range(1, PASSES):
+                w1_w[e, s] = words[:, s - 1, :]
 
         first_rows = xT[0:K_PASS, :].rearrange("(p j) t -> p j t", j=PACK)
         for i in range(2):
@@ -92,18 +99,17 @@ def tile_moe_ecr_mlp_silu_kernel(
         load_tokens(1)
         load_tokens(2)
         nc.sync.dma_start(pos_t[0][:], pos1)
-        load_scale_rows(w1_sc[0], w1_scales[0:W2_GROUP])
-        load_w1(0, 2)
-        load_w1(2, 4)
-        load_scale_rows(w1_sc[1], w1_scales[W2_GROUP:E])
-        load_w1(4, 6)
-        load_w1(6, 8)
+        for g, e0 in enumerate(range(0, E, W2_GROUP)):
+            load_scale_rows(w1_sc[g], w1_scales[e0:e0 + W2_GROUP])
+            load_w1_first(e0)
+            for e in range(e0, e0 + W2_GROUP):
+                load_w1_rest(e)
         load_scale_rows(w2_sc, w2_scales)
         nc.sync.dma_start(w2_w[:].bitcast(I32), w2_words.rearrange("e s p b -> p (e s) b").bitcast(I32))
-        for r, pos in ((1, pos2), (2, pos3), (3, pos4)):
+        for r, pos in ((3, pos4), (2, pos3), (1, pos2)):
             nc.sync.dma_start(pos_t[r][:], pos)
-        for r in (2, 0):
-            nc.sync.dma_start(gate_t[:, r:r + 2, :], gate[r:r + 2, 0:P, :].rearrange("r p t -> p r t"))
+        for r in range(TOP - 1, -1, -1):
+            nc.sync.dma_start(gate_t[r][:], gate[r, 0:P, :])
 
         x_bf = [keep.tile([P, T, PACK], BF16, name="x_bf%d" % s, align_bytes=64) for s in range(PASSES)]
         x_w12 = keep.tile([P, 2 * T], U32, name="x_w12", align_bytes=64)
@@ -135,22 +141,24 @@ def tile_moe_ecr_mlp_silu_kernel(
 
         def first_product(s, e, start, stop):
             slots = slice(e * C, (e + 1) * C)
-            words, row = w1_w[e]
             g = (e % W2_GROUP) * PASSES + s
             nc.tensor.matmul_mx(
                 out=bank[e][:],
                 lhsT=g_w[s][:, slots].bitcast(FP8X4),
                 lhsT_scale=g_sc[s][:, slots],
-                rhs=words[:, row + s, :].bitcast(FP4X4),
+                rhs=w1_w[e, s].bitcast(FP4X4),
                 rhs_scale=w1_sc[e // W2_GROUP][:, g * H:(g + 1) * H],
                 start=start,
                 stop=stop,
             )
 
         def first_products(e0, e1):
-            for s in range(PASSES):
+            if e0 % W2_GROUP == 0:
+                for e in range(e0, e0 + W2_GROUP):
+                    first_product(0, e, True, False)
+            for s in range(1, PASSES):
                 for e in range(e0, e1):
-                    first_product(s, e, s == 0, s == PASSES - 1)
+                    first_product(s, e, False, s == PASSES - 1)
 
         h_bf = {}
 
@@ -235,7 +243,7 @@ def tile_moe_ecr_mlp_silu_kernel(
 
         def weighted(hf, r):
             prod[hf, r] = keep.tile([P, T], F32, name="prod%d_%d" % (hf, r))
-            nc.vector.tensor_tensor(prod[hf, r][:], y[hf][:].indirect(pos_t[r][:]), gate_t[:, r, :], MULT)
+            nc.vector.tensor_tensor(prod[hf, r][:], y[hf][:].indirect(pos_t[r][:]), gate_t[r][:], MULT)
 
         back = {}
         SUM_BANKS = ((2, 3, 4, 5), (0, 6, 1, 7))
@@ -258,7 +266,7 @@ def tile_moe_ecr_mlp_silu_kernel(
         for hf, t0, t1 in ((0, 0, T), (1, 0, T // 2), (1, T // 2, T)):
             last = keep.tile([P, t1 - t0], F32, name="last%d_%d" % (hf, t0))
             nc.vector.tensor_tensor(
-                last[:], y[hf][:].indirect(pos_t[0][:, t0 // 16:t1 // 16]), gate_t[:, 0, t0:t1], MULT
+                last[:], y[hf][:].indirect(pos_t[0][:, t0 // 16:t1 // 16]), gate_t[0][:, t0:t1], MULT
             )
             total = keep.tile([P, t1 - t0], F32, name="total%d_%d" % (hf, t0))
             nc.vector.tensor_tensor(total[:], back[hf][:, t0:t1], last[:], ADD)

@@ -30,6 +30,8 @@ PAIR = 2 * C
 VEC_TOKENS = 160
 W2_GROUP = 4
 SPARE = 192
+VEC_TAIL = 128
+SHIFT_ROWS = 112
 
 
 def tile_moe_ecr_mlp_silu_kernel(
@@ -43,15 +45,17 @@ def tile_moe_ecr_mlp_silu_kernel(
 
         w1_sc = [keep.tile([P, W2_GROUP * PASSES * H], U8, name="w1_sc%d" % g, align_bytes=64) for g in range(E // W2_GROUP)]
         w2_sc = keep.tile([P, E * N], U8, name="w2_sc", align_bytes=64)
-        x_sc0 = keep.tile([P, T + SPARE], U8, name="x_sc0", align_bytes=64)
+        x_sc01 = keep.tile([P, T + SPARE], U8, name="x_sc01", align_bytes=64)
         x_w0 = keep.tile([P, T + SPARE], I32, name="x_w0", align_bytes=64)
-        x_sc12 = keep.tile([P, 2 * T], U8, name="x_sc12", align_bytes=64)
+        x_sc2 = keep.tile([P, T], U8, name="x_sc2", align_bytes=64)
+        g_sc1 = keep.tile([P, S], U8, name="g_sc1", align_bytes=64)
         zeros = keep.tile([P, PAD], F32, name="zeros")
         nc.vector.memset(zeros[:], 0.0)
         nc.vector.memset(x_w0[:, T:], 0)
-        for plane in (x_sc0, w1_sc[0], x_sc12, w1_sc[1]):
+        for plane in (x_sc01, w1_sc[0], x_sc2, w1_sc[1]):
             nc.vector.memset(plane[:].bitcast(I32), 0)
-        nc.gpsimd.memset(w2_sc[:].bitcast(I32), 0)
+        for plane in (g_sc1, w2_sc):
+            nc.gpsimd.memset(plane[:].bitcast(I32), 0)
         ident = keep.tile([P, P], F32, name="ident")
         make_identity(nc, ident[:])
 
@@ -64,7 +68,7 @@ def tile_moe_ecr_mlp_silu_kernel(
         offs_t = keep.tile([P, S // 16], U16, name="offs_t")
         pos_t = [keep.tile([P, T // 16], U16, name="pos_t%d" % r) for r in range(TOP)]
         w2_w = keep.tile([P, E, 2 * N], U8, name="w2_w", align_bytes=64)
-        gate_t = [keep.tile([P, T], F32, name="gate_t%d" % r) for r in range(TOP)]
+        gate_t = keep.tile([P, TOP, T], F32, name="gate_t")
         w1_w = {}
 
         def load_tokens(s):
@@ -92,6 +96,13 @@ def tile_moe_ecr_mlp_silu_kernel(
             for s in range(1, PASSES):
                 w1_w[e, s] = words[:, s - 1, :]
 
+        def load_w1_pair(e0):
+            words = keep.tile([P, 2 * PASSES, 2 * H], U8, name="w1_pair%d" % e0, align_bytes=64)
+            nc.sync.dma_start(words[:].bitcast(I32), w1_words[e0:e0 + 2].rearrange("e s p b -> p (e s) b").bitcast(I32))
+            for e in range(e0, e0 + 2):
+                for s in range(PASSES):
+                    w1_w[e, s] = words[:, (e - e0) * PASSES + s, :]
+
         first_rows = xT[0:K_PASS, :].rearrange("(p j) t -> p j t", j=PACK)
         for i in range(2):
             nc.sync.dma_start(x_first[i][:], first_rows[:, :, i * T // 2:(i + 1) * T // 2])
@@ -99,22 +110,24 @@ def tile_moe_ecr_mlp_silu_kernel(
         load_tokens(1)
         load_tokens(2)
         nc.sync.dma_start(pos_t[0][:], pos1)
-        for g, e0 in enumerate(range(0, E, W2_GROUP)):
-            load_scale_rows(w1_sc[g], w1_scales[e0:e0 + W2_GROUP])
-            load_w1_first(e0)
-            for e in range(e0, e0 + W2_GROUP):
-                load_w1_rest(e)
+        load_scale_rows(w1_sc[0], w1_scales[0:W2_GROUP])
+        load_w1_first(0)
+        for e in range(W2_GROUP):
+            load_w1_rest(e)
+        load_scale_rows(w1_sc[1], w1_scales[W2_GROUP:E])
+        for e0 in range(W2_GROUP, E, 2):
+            load_w1_pair(e0)
         load_scale_rows(w2_sc, w2_scales)
         nc.sync.dma_start(w2_w[:].bitcast(I32), w2_words.rearrange("e s p b -> p (e s) b").bitcast(I32))
         for r, pos in ((3, pos4), (2, pos3), (1, pos2)):
             nc.sync.dma_start(pos_t[r][:], pos)
-        for r in range(TOP - 1, -1, -1):
-            nc.sync.dma_start(gate_t[r][:], gate[r, 0:P, :])
+        for r in (2, 0):
+            nc.sync.dma_start(gate_t[:, r:r + 2, :], gate[r:r + 2, 0:P, :].rearrange("r p t -> p r t"))
 
         x_bf = [keep.tile([P, T, PACK], BF16, name="x_bf%d" % s, align_bytes=64) for s in range(PASSES)]
         x_w12 = keep.tile([P, 2 * T], U32, name="x_w12", align_bytes=64)
         x_w = [x_w0[:, 0:T].bitcast(U32), x_w12[:, 0:T], x_w12[:, T:2 * T]]
-        x_sc = [x_sc0[:, 0:T], x_sc12[:, 0:T], x_sc12[:, T:2 * T]]
+        x_sc = [x_sc01[:, 0:T], x_sc01[4:P, 0:T], x_sc2[:]]
 
         def cast(engine, s, raw, t0):
             dst = x_bf[s][:, t0:t0 + raw.shape[2], :].rearrange("p (c i) j -> p c j i", i=4)
@@ -132,7 +145,8 @@ def tile_moe_ecr_mlp_silu_kernel(
             )
 
         g_w = [keep.tile([P, S], U32, name="g_w%d" % s, align_bytes=64) for s in range(PASSES)]
-        g_sc = [keep.tile([P, S], U8, name="g_sc%d" % s, align_bytes=64) for s in range(PASSES)]
+        g_sc01 = keep.tile([P, S], U8, name="g_sc01", align_bytes=64)
+        g_sc = [g_sc01, g_sc1, keep.tile([P, S], U8, name="g_sc2", align_bytes=64)]
 
         def gather(dst, window, e0, e1):
             nc.vector.tensor_copy(dst[:, e0 * C:e1 * C], window.indirect(offs_t[:, e0 * C // 16:e1 * C // 16]))
@@ -153,12 +167,13 @@ def tile_moe_ecr_mlp_silu_kernel(
             )
 
         def first_products(e0, e1):
-            if e0 % W2_GROUP == 0:
-                for e in range(e0, e0 + W2_GROUP):
+            if e0 != 2:
+                for e in range(e0, W2_GROUP if e0 == 0 else e1):
                     first_product(0, e, True, False)
-            for s in range(1, PASSES):
+            order = (2, 1) if e0 == 0 else (1, 2)
+            for s in order:
                 for e in range(e0, e1):
-                    first_product(s, e, False, s == PASSES - 1)
+                    first_product(s, e, False, s == order[-1])
 
         h_bf = {}
 
@@ -173,7 +188,7 @@ def tile_moe_ecr_mlp_silu_kernel(
             for u in range(2):
                 nc.tensor.transpose(bank[e][:, u * C:(u + 1) * C], words[:, u * P:(u + 1) * P], ident[:])
             h_bf[e] = keep.tile([P, C * PACK], BF16, name="h_bf%d" % e, align_bytes=64)
-            copy = nc.vector.tensor_copy if e in (E - 4, E - 3) else nc.scalar.copy
+            copy = nc.vector.tensor_copy if 2 <= e < E - 2 else nc.scalar.copy
             copy(
                 h_bf[e][:].bitcast(F32).rearrange("p (c u) -> p c u", u=2),
                 bank[e][:, 0:2 * C].rearrange("p (u c) -> p c u", u=2),
@@ -210,19 +225,21 @@ def tile_moe_ecr_mlp_silu_kernel(
         quantise_tokens(0, half, T)
         for e0 in range(0, E, 4):
             gather(g_w[0], x_w0[:].bitcast(U32), e0, e0 + 4)
-            gather(g_sc[0], x_sc0[:], e0, e0 + 4)
-        cast("scalar", 1, x_raw[1][:], 0)
+        cast("scalar", 1, x_raw[1][:, :, 0:T - VEC_TAIL], 0)
+        cast("vector", 1, x_raw[1][:, :, T - VEC_TAIL:T], T - VEC_TAIL)
         quantise_tokens(1, 0, T)
+        for e0 in range(0, E, 4):
+            gather(g_sc01, x_sc01[:], e0, e0 + 4)
+            cols = slice(e0 * C, (e0 + 4) * C)
+            nc.gpsimd.dma_start(g_sc1[0:SHIFT_ROWS, cols].bitcast(I32), g_sc01[4:4 + SHIFT_ROWS, cols].bitcast(I32))
         gather(g_w[1], x_w[1], 0, 2)
-        gather(g_sc[1], x_sc[1], 0, 2)
         cast("scalar", 2, x_raw[2][:], 0)
         quantise_tokens(2, 0, T)
         for e0, e1 in STEPS:
             if e0 > 0 and e0 % 2 == 0:
                 gather(g_w[1], x_w12[:], e0, e0 + 2)
-                gather(g_sc[1], x_sc12[:], e0, e0 + 2)
             gather(g_w[2], x_w[2], e0, e1)
-            gather(g_sc[2], x_sc[2], e0, e1)
+            gather(g_sc[2], x_sc2[:], e0, e1)
         for e0 in range(0, E, 2):
             first_products(e0, e0 + 2)
             for e in range(max(e0 - 2, 0), e0):
@@ -243,7 +260,7 @@ def tile_moe_ecr_mlp_silu_kernel(
 
         def weighted(hf, r):
             prod[hf, r] = keep.tile([P, T], F32, name="prod%d_%d" % (hf, r))
-            nc.vector.tensor_tensor(prod[hf, r][:], y[hf][:].indirect(pos_t[r][:]), gate_t[r][:], MULT)
+            nc.vector.tensor_tensor(prod[hf, r][:], y[hf][:].indirect(pos_t[r][:]), gate_t[:, r, :], MULT)
 
         back = {}
         SUM_BANKS = ((2, 3, 4, 5), (0, 6, 1, 7))
@@ -266,7 +283,7 @@ def tile_moe_ecr_mlp_silu_kernel(
         for hf, t0, t1 in ((0, 0, T), (1, 0, T // 2), (1, T // 2, T)):
             last = keep.tile([P, t1 - t0], F32, name="last%d_%d" % (hf, t0))
             nc.vector.tensor_tensor(
-                last[:], y[hf][:].indirect(pos_t[0][:, t0 // 16:t1 // 16]), gate_t[0][:, t0:t1], MULT
+                last[:], y[hf][:].indirect(pos_t[0][:, t0 // 16:t1 // 16]), gate_t[:, 0, t0:t1], MULT
             )
             total = keep.tile([P, t1 - t0], F32, name="total%d_%d" % (hf, t0))
             nc.vector.tensor_tensor(total[:], back[hf][:, t0:t1], last[:], ADD)

@@ -26,12 +26,17 @@ PACK = 4
 K_PASS = P * PACK
 PASSES = K // K_PASS
 HALVES = N // P
-PAIR = 2 * C
-VEC_TOKENS = 160
-W2_GROUP = 4
+PER_COLUMN = 16
+LIVE = 4
+QUAD = 4
 SPARE = 192
-VEC_TAIL = 128
-SHIFT_ROWS = 112
+SHIFT_ROWS = 3 * 32 + LIVE
+
+VECTOR_SHARE_PASS0 = 160
+VECTOR_SHARE_PASS1 = 128
+
+STEPS = ((0, 2), (2, 4), (4, 6), (6, 7), (7, 8))
+SUM_BANKS = ((2, 3, 4, 5), (0, 6, 1, 7))
 
 
 def tile_moe_ecr_mlp_silu_kernel(
@@ -43,7 +48,7 @@ def tile_moe_ecr_mlp_silu_kernel(
         ring = ctx.enter_context(tc.tile_pool(name="ring", bufs=3))
         psum = ctx.enter_context(tc.psum_pool(name="psum", bufs=1))
 
-        w1_sc = [keep.tile([P, W2_GROUP * PASSES * H], U8, name="w1_sc%d" % g, align_bytes=64) for g in range(E // W2_GROUP)]
+        w1_sc = [keep.tile([P, QUAD * PASSES * H], U8, name="w1_sc%d" % g, align_bytes=64) for g in range(E // QUAD)]
         w2_sc = keep.tile([P, E * N], U8, name="w2_sc", align_bytes=64)
         x_sc01 = keep.tile([P, T + SPARE], U8, name="x_sc01", align_bytes=64)
         x_w0 = keep.tile([P, T + SPARE], I32, name="x_w0", align_bytes=64)
@@ -65,29 +70,27 @@ def tile_moe_ecr_mlp_silu_kernel(
 
         x_first = [keep.tile([P, PACK, T // 2], F32, name="x_first%d" % i) for i in range(2)]
         x_raw = {s: keep.tile([P, PACK, T], F32, name="x_raw%d" % s) for s in range(1, PASSES)}
-        offs_t = keep.tile([P, S // 16], U16, name="offs_t")
-        pos_t = [keep.tile([P, T // 16], U16, name="pos_t%d" % r) for r in range(TOP)]
+        offs_t = keep.tile([P, S // PER_COLUMN], U16, name="offs_t")
+        pos_t = [keep.tile([P, T // PER_COLUMN], U16, name="pos_t%d" % r) for r in range(TOP)]
         w2_w = keep.tile([P, E, 2 * N], U8, name="w2_w", align_bytes=64)
         gate_t = keep.tile([P, TOP, T], F32, name="gate_t")
         w1_w = {}
 
-        def load_tokens(s):
-            rows = xT[s * K_PASS:(s + 1) * K_PASS, :].rearrange("(p j) t -> p j t", j=PACK)
-            for j in (0, 2):
-                nc.sync.dma_start(x_raw[s][:, j:j + 2, :], rows[:, j:j + 2, :])
+        def token_rows(s):
+            return xT[s * K_PASS:(s + 1) * K_PASS, :].rearrange("(p j) t -> p j t", j=PACK)
 
         def load_scale_rows(plane, scales):
-            rows = scales.rearrange("e s (q r) i -> r q (e s) i", r=4)
-            for r in range(4):
+            rows = scales.rearrange("e s (q r) i -> r q (e s) i", r=LIVE)
+            for r in range(LIVE):
                 nc.sync.dma_start(
                     plane[r:P:32, :].bitcast(I32).rearrange("q (g i) -> q g i", g=rows.shape[2]), rows[r].bitcast(I32)
                 )
 
         def load_w1_first(e0):
-            words = keep.tile([P, W2_GROUP, 2 * H], U8, name="w1_first%d" % e0, align_bytes=64)
-            src = w1_words[e0:e0 + W2_GROUP, 0].rearrange("e p b -> p e b")
+            words = keep.tile([P, QUAD, 2 * H], U8, name="w1_first%d" % e0, align_bytes=64)
+            src = w1_words[e0:e0 + QUAD, 0].rearrange("e p b -> p e b")
             nc.sync.dma_start(words[:].bitcast(I32), src.bitcast(I32))
-            for e in range(e0, e0 + W2_GROUP):
+            for e in range(e0, e0 + QUAD):
                 w1_w[e, 0] = words[:, e - e0, :]
 
         def load_w1_rest(e):
@@ -103,19 +106,19 @@ def tile_moe_ecr_mlp_silu_kernel(
                 for s in range(PASSES):
                     w1_w[e, s] = words[:, (e - e0) * PASSES + s, :]
 
-        first_rows = xT[0:K_PASS, :].rearrange("(p j) t -> p j t", j=PACK)
         for i in range(2):
-            nc.sync.dma_start(x_first[i][:], first_rows[:, :, i * T // 2:(i + 1) * T // 2])
+            nc.sync.dma_start(x_first[i][:], token_rows(0)[:, :, i * T // 2:(i + 1) * T // 2])
         nc.sync.dma_start(offs_t[:], offs)
-        load_tokens(1)
-        load_tokens(2)
+        for s in range(1, PASSES):
+            for j in (0, 2):
+                nc.sync.dma_start(x_raw[s][:, j:j + 2, :], token_rows(s)[:, j:j + 2, :])
         nc.sync.dma_start(pos_t[0][:], pos1)
-        load_scale_rows(w1_sc[0], w1_scales[0:W2_GROUP])
+        load_scale_rows(w1_sc[0], w1_scales[0:QUAD])
         load_w1_first(0)
-        for e in range(W2_GROUP):
+        for e in range(QUAD):
             load_w1_rest(e)
-        load_scale_rows(w1_sc[1], w1_scales[W2_GROUP:E])
-        for e0 in range(W2_GROUP, E, 2):
+        load_scale_rows(w1_sc[1], w1_scales[QUAD:E])
+        for e0 in range(QUAD, E, 2):
             load_w1_pair(e0)
         load_scale_rows(w2_sc, w2_scales)
         nc.sync.dma_start(w2_w[:].bitcast(I32), w2_words.rearrange("e s p b -> p (e s) b").bitcast(I32))
@@ -127,15 +130,14 @@ def tile_moe_ecr_mlp_silu_kernel(
         x_bf = [keep.tile([P, T, PACK], BF16, name="x_bf%d" % s, align_bytes=64) for s in range(PASSES)]
         x_w12 = keep.tile([P, 2 * T], U32, name="x_w12", align_bytes=64)
         x_w = [x_w0[:, 0:T].bitcast(U32), x_w12[:, 0:T], x_w12[:, T:2 * T]]
-        x_sc = [x_sc01[:, 0:T], x_sc01[4:P, 0:T], x_sc2[:]]
+        x_sc = [x_sc01[:, 0:T], x_sc01[LIVE:P, 0:T], x_sc2[:]]
 
-        def cast(engine, s, raw, t0):
+        def scalar_copy(dst, src):
+            nc.scalar.activation(dst, src, COPY)
+
+        def round_tokens(copy, s, raw, t0):
             dst = x_bf[s][:, t0:t0 + raw.shape[2], :].rearrange("p (c i) j -> p c j i", i=4)
-            src = raw.rearrange("p j (c i) -> p c j i", i=4)
-            if engine == "vector":
-                nc.vector.tensor_copy(dst, src)
-            else:
-                nc.scalar.activation(dst, src, COPY)
+            copy(dst, raw.rearrange("p j (c i) -> p c j i", i=4))
 
         def quantise_tokens(s, t0, t1):
             nc.vector.quantize_mx(
@@ -149,30 +151,31 @@ def tile_moe_ecr_mlp_silu_kernel(
         g_sc = [g_sc01, g_sc1, keep.tile([P, S], U8, name="g_sc2", align_bytes=64)]
 
         def gather(dst, window, e0, e1):
-            nc.vector.tensor_copy(dst[:, e0 * C:e1 * C], window.indirect(offs_t[:, e0 * C // 16:e1 * C // 16]))
+            entries = offs_t[:, e0 * C // PER_COLUMN:e1 * C // PER_COLUMN]
+            nc.vector.tensor_copy(dst[:, e0 * C:e1 * C], window.indirect(entries))
 
         bank = [psum.tile([P, H], F32, name="bank%d" % e) for e in range(E)]
 
         def first_product(s, e, start, stop):
             slots = slice(e * C, (e + 1) * C)
-            g = (e % W2_GROUP) * PASSES + s
+            place = (e % QUAD) * PASSES + s
             nc.tensor.matmul_mx(
                 out=bank[e][:],
                 lhsT=g_w[s][:, slots].bitcast(FP8X4),
                 lhsT_scale=g_sc[s][:, slots],
                 rhs=w1_w[e, s].bitcast(FP4X4),
-                rhs_scale=w1_sc[e // W2_GROUP][:, g * H:(g + 1) * H],
+                rhs_scale=w1_sc[e // QUAD][:, place * H:(place + 1) * H],
                 start=start,
                 stop=stop,
             )
 
-        def first_products(e0, e1):
-            if e0 != 2:
-                for e in range(e0, W2_GROUP if e0 == 0 else e1):
-                    first_product(0, e, True, False)
-            order = (2, 1) if e0 == 0 else (1, 2)
+        def open_sums(e0, e1):
+            for e in range(e0, e1):
+                first_product(0, e, True, False)
+
+        def close_sums(e0, order):
             for s in order:
-                for e in range(e0, e1):
+                for e in (e0, e0 + 1):
                     first_product(s, e, False, s == order[-1])
 
         h_bf = {}
@@ -184,9 +187,9 @@ def tile_moe_ecr_mlp_silu_kernel(
                 bank[e][:].rearrange("c (p u d) -> c u p d", u=2, d=2),
                 SILU,
             )
-            words = h_t[:].bitcast(F32)
+            pairs = h_t[:].bitcast(F32)
             for u in range(2):
-                nc.tensor.transpose(bank[e][:, u * C:(u + 1) * C], words[:, u * P:(u + 1) * P], ident[:])
+                nc.tensor.transpose(bank[e][:, u * C:(u + 1) * C], pairs[:, u * P:(u + 1) * P], ident[:])
             h_bf[e] = keep.tile([P, C * PACK], BF16, name="h_bf%d" % e, align_bytes=64)
             copy = nc.vector.tensor_copy if 2 <= e < E - 2 else nc.scalar.copy
             copy(
@@ -216,32 +219,41 @@ def tile_moe_ecr_mlp_silu_kernel(
                 )
             copy(y[hf][:, e0 * C:e1 * C], acc[:, 0:(e1 - e0) * C])
 
-        STEPS = ((0, 2), (2, 4), (4, 6), (6, 7), (7, 8))
-        half = T // 2
-        cast("vector", 0, x_first[0][:], 0)
-        quantise_tokens(0, 0, half)
-        cast("vector", 0, x_first[1][:, :, 0:VEC_TOKENS], half)
-        cast("scalar", 0, x_first[1][:, :, VEC_TOKENS:half], half + VEC_TOKENS)
-        quantise_tokens(0, half, T)
-        for e0 in range(0, E, 4):
-            gather(g_w[0], x_w0[:].bitcast(U32), e0, e0 + 4)
-        cast("scalar", 1, x_raw[1][:, :, 0:T - VEC_TAIL], 0)
-        cast("vector", 1, x_raw[1][:, :, T - VEC_TAIL:T], T - VEC_TAIL)
+        middle = T // 2
+        round_tokens(nc.vector.tensor_copy, 0, x_first[0][:], 0)
+        quantise_tokens(0, 0, middle)
+        round_tokens(nc.vector.tensor_copy, 0, x_first[1][:, :, 0:VECTOR_SHARE_PASS0], middle)
+        round_tokens(scalar_copy, 0, x_first[1][:, :, VECTOR_SHARE_PASS0:middle], middle + VECTOR_SHARE_PASS0)
+        quantise_tokens(0, middle, T)
+        for e0 in range(0, E, QUAD):
+            gather(g_w[0], x_w0[:].bitcast(U32), e0, e0 + QUAD)
+
+        split = T - VECTOR_SHARE_PASS1
+        round_tokens(scalar_copy, 1, x_raw[1][:, :, 0:split], 0)
+        round_tokens(nc.vector.tensor_copy, 1, x_raw[1][:, :, split:T], split)
         quantise_tokens(1, 0, T)
-        for e0 in range(0, E, 4):
-            gather(g_sc01, x_sc01[:], e0, e0 + 4)
-            cols = slice(e0 * C, (e0 + 4) * C)
-            nc.gpsimd.dma_start(g_sc1[0:SHIFT_ROWS, cols].bitcast(I32), g_sc01[4:4 + SHIFT_ROWS, cols].bitcast(I32))
+        for e0 in range(0, E, QUAD):
+            gather(g_sc01, x_sc01[:], e0, e0 + QUAD)
+            cols = slice(e0 * C, (e0 + QUAD) * C)
+            nc.gpsimd.dma_start(
+                g_sc1[0:SHIFT_ROWS, cols].bitcast(I32), g_sc01[LIVE:LIVE + SHIFT_ROWS, cols].bitcast(I32)
+            )
         gather(g_w[1], x_w[1], 0, 2)
-        cast("scalar", 2, x_raw[2][:], 0)
+
+        round_tokens(scalar_copy, 2, x_raw[2][:], 0)
         quantise_tokens(2, 0, T)
         for e0, e1 in STEPS:
             if e0 > 0 and e0 % 2 == 0:
                 gather(g_w[1], x_w12[:], e0, e0 + 2)
             gather(g_w[2], x_w[2], e0, e1)
             gather(g_sc[2], x_sc2[:], e0, e1)
+
         for e0 in range(0, E, 2):
-            first_products(e0, e0 + 2)
+            if e0 == 0:
+                open_sums(0, QUAD)
+            if e0 >= QUAD:
+                open_sums(e0, e0 + 2)
+            close_sums(e0, (2, 1) if e0 == 0 else (1, 2))
             for e in range(max(e0 - 2, 0), e0):
                 hidden(e)
                 quantise_hidden(e)
@@ -249,29 +261,26 @@ def tile_moe_ecr_mlp_silu_kernel(
             hidden(e)
         for e in (E - 2, E - 1):
             quantise_hidden(e)
-        second_products(0, 0, 4, 6, nc.scalar.copy)
-        second_products(0, 6, 7, 0, nc.vector.tensor_copy)
-        second_products(0, 4, 6, 7, nc.scalar.copy)
-        second_products(0, 7, 8, 1, nc.vector.tensor_copy)
-        second_products(1, 0, 4, 1, nc.scalar.copy)
-        second_products(1, 4, 8, 7, nc.scalar.copy)
 
-        prod = {}
-
-        def weighted(hf, r):
-            prod[hf, r] = keep.tile([P, T], F32, name="prod%d_%d" % (hf, r))
-            nc.vector.tensor_tensor(prod[hf, r][:], y[hf][:].indirect(pos_t[r][:]), gate_t[:, r, :], MULT)
+        second_products(0, 0, QUAD, E - 2, nc.scalar.copy)
+        second_products(0, E - 2, E - 1, 0, nc.vector.tensor_copy)
+        second_products(0, QUAD, E - 2, E - 1, nc.scalar.copy)
+        second_products(0, E - 1, E, 1, nc.vector.tensor_copy)
+        second_products(1, 0, QUAD, 1, nc.scalar.copy)
+        second_products(1, QUAD, E, E - 1, nc.scalar.copy)
 
         back = {}
-        SUM_BANKS = ((2, 3, 4, 5), (0, 6, 1, 7))
         chunks = T // P
         for hf in range(HALVES):
-            sums = [psum.tile([P, H], F32, name="sums%d_%d" % (hf, c), tag="bank%d" % SUM_BANKS[hf][c]) for c in range(chunks)]
+            sums = [
+                psum.tile([P, H], F32, name="sums%d_%d" % (hf, c), tag="bank%d" % SUM_BANKS[hf][c]) for c in range(chunks)
+            ]
             for r in range(TOP - 1, 0, -1):
-                weighted(hf, r)
+                prod = keep.tile([P, T], F32, name="prod%d_%d" % (hf, r))
+                nc.vector.tensor_tensor(prod[:], y[hf][:].indirect(pos_t[r][:]), gate_t[:, r, :], MULT)
                 for c in range(chunks):
                     nc.tensor.matmul(
-                        sums[c][:, 0:P], prod[hf, r][:, c * P:(c + 1) * P], ident[:],
+                        sums[c][:, 0:P], prod[:, c * P:(c + 1) * P], ident[:],
                         start=(r == TOP - 1), stop=(r == 1), is_transpose=True,
                     )
             turned = keep.tile([P, T], F32, name="turned%d" % hf)
@@ -280,11 +289,10 @@ def tile_moe_ecr_mlp_silu_kernel(
             back[hf] = psum.tile([P, H], F32, name="back%d" % hf, tag="bank%d" % SUM_BANKS[hf][0])
             for c in range(chunks):
                 nc.tensor.transpose(back[hf][:, c * P:(c + 1) * P], turned[:, c * P:(c + 1) * P], ident[:])
-        for hf, t0, t1 in ((0, 0, T), (1, 0, T // 2), (1, T // 2, T)):
+        for hf, t0, t1 in ((0, 0, T), (1, 0, middle), (1, middle, T)):
             last = keep.tile([P, t1 - t0], F32, name="last%d_%d" % (hf, t0))
-            nc.vector.tensor_tensor(
-                last[:], y[hf][:].indirect(pos_t[0][:, t0 // 16:t1 // 16]), gate_t[:, 0, t0:t1], MULT
-            )
+            entries = pos_t[0][:, t0 // PER_COLUMN:t1 // PER_COLUMN]
+            nc.vector.tensor_tensor(last[:], y[hf][:].indirect(entries), gate_t[:, 0, t0:t1], MULT)
             total = keep.tile([P, t1 - t0], F32, name="total%d_%d" % (hf, t0))
             nc.vector.tensor_tensor(total[:], back[hf][:, t0:t1], last[:], ADD)
             nc.sync.dma_start(out[hf * P:(hf + 1) * P, t0:t1], total[:])

from contextlib import ExitStack

import concourse.mybir as mybir
from concourse.masks import make_identity

K, T, E, C, H, N = 1536, 512, 8, 128, 512, 256
TOP, PAD = 4, 64
S = E * C
FLOPS = 2 * S * (K * H + H * N)

F32 = mybir.dt.float32
BF16 = mybir.dt.bfloat16
I32 = mybir.dt.int32
U32 = mybir.dt.uint32
U16 = mybir.dt.uint16
U8 = mybir.dt.uint8
FP8X4 = mybir.dt.float8_e4m3fn_x4
FP4X4 = mybir.dt.float4_e2m1fn_x4
COPY = mybir.ActivationFunctionType.Copy
SILU = mybir.ActivationFunctionType.Silu
MULT = mybir.AluOpType.mult
ADD = mybir.AluOpType.add

P = 128
PACK = 4
K_PASS = P * PACK
PASSES = K // K_PASS
HALVES = N // P
PER_COLUMN = 16
LIVE = 4
QUAD = 4
SPARE = 192
SHIFT_ROWS = 3 * 32 + LIVE

VECTOR_SHARE_PASS0 = 160
VECTOR_SHARE_PASS1 = 128

STEPS = ((0, 2), (2, 4), (4, 6), (6, 7), (7, 8))
SUM_BANKS = ((2, 3, 4, 5), (0, 6, 1, 7))


def tile_moe_ecr_mlp_silu_kernel(
    tc, xT, w1_words, w1_scales, w2_words, w2_scales, gate, offs, pos1, pos2, pos3, pos4, out
):
    nc = tc.nc
    with ExitStack() as ctx:
        keep = ctx.enter_context(tc.tile_pool(name="keep", bufs=1))
        ring = ctx.enter_context(tc.tile_pool(name="ring", bufs=3))
        psum = ctx.enter_context(tc.psum_pool(name="psum", bufs=1))

        w1_sc = [keep.tile([P, QUAD * PASSES * H], U8, name="w1_sc%d" % g, align_bytes=64) for g in range(E // QUAD)]
        w2_sc = keep.tile([P, E * N], U8, name="w2_sc", align_bytes=64)
        x_sc01 = keep.tile([P, T + SPARE], U8, name="x_sc01", align_bytes=64)
        x_w0 = keep.tile([P, T + SPARE], I32, name="x_w0", align_bytes=64)
        x_sc2 = keep.tile([P, T], U8, name="x_sc2", align_bytes=64)
        g_sc1 = keep.tile([P, S], U8, name="g_sc1", align_bytes=64)
        zeros = keep.tile([P, PAD], F32, name="zeros")
        nc.vector.memset(zeros[:], 0.0)
        nc.vector.memset(x_w0[:, T:], 0)
        for plane in (x_sc01, w1_sc[0], x_sc2, w1_sc[1]):
            nc.vector.memset(plane[:].bitcast(I32), 0)
        for plane in (g_sc1, w2_sc):
            nc.gpsimd.memset(plane[:].bitcast(I32), 0)
        ident = keep.tile([P, P], F32, name="ident")
        make_identity(nc, ident[:])

        y = [keep.tile([P, S + PAD], F32, name="y%d" % hf) for hf in range(HALVES)]
        for hf in range(HALVES):
            nc.scalar.activation(y[hf][:, S:], zeros[:], SILU)

        x_first = [keep.tile([P, PACK, T // 2], F32, name="x_first%d" % i) for i in range(2)]
        x_raw = {s: keep.tile([P, PACK, T], F32, name="x_raw%d" % s) for s in range(1, PASSES)}
        offs_t = keep.tile([P, S // PER_COLUMN], U16, name="offs_t")
        pos_t = [keep.tile([P, T // PER_COLUMN], U16, name="pos_t%d" % r) for r in range(TOP)]
        w2_w = keep.tile([P, E, 2 * N], U8, name="w2_w", align_bytes=64)
        gate_t = keep.tile([P, TOP, T], F32, name="gate_t")
        w1_w = {}

        def token_rows(s):
            return xT[s * K_PASS:(s + 1) * K_PASS, :].rearrange("(p j) t -> p j t", j=PACK)

        def load_scale_rows(plane, scales):
            rows = scales.rearrange("e s (q r) i -> r q (e s) i", r=LIVE)
            for r in range(LIVE):
                nc.sync.dma_start(
                    plane[r:P:32, :].bitcast(I32).rearrange("q (g i) -> q g i", g=rows.shape[2]), rows[r].bitcast(I32)
                )

        def load_w1_first(e0):
            words = keep.tile([P, QUAD, 2 * H], U8, name="w1_first%d" % e0, align_bytes=64)
            src = w1_words[e0:e0 + QUAD, 0].rearrange("e p b -> p e b")
            nc.sync.dma_start(words[:].bitcast(I32), src.bitcast(I32))
            for e in range(e0, e0 + QUAD):
                w1_w[e, 0] = words[:, e - e0, :]

        def load_w1_rest(e):
            words = keep.tile([P, PASSES - 1, 2 * H], U8, name="w1_rest%d" % e, align_bytes=64)
            nc.sync.dma_start(words[:].bitcast(I32), w1_words[e, 1:PASSES].rearrange("s p b -> p s b").bitcast(I32))
            for s in range(1, PASSES):
                w1_w[e, s] = words[:, s - 1, :]

        def load_w1_pair(e0):
            words = keep.tile([P, 2 * PASSES, 2 * H], U8, name="w1_pair%d" % e0, align_bytes=64)
            nc.sync.dma_start(words[:].bitcast(I32), w1_words[e0:e0 + 2].rearrange("e s p b -> p (e s) b").bitcast(I32))
            for e in range(e0, e0 + 2):
                for s in range(PASSES):
                    w1_w[e, s] = words[:, (e - e0) * PASSES + s, :]

        for i in range(2):
            nc.sync.dma_start(x_first[i][:], token_rows(0)[:, :, i * T // 2:(i + 1) * T // 2])
        nc.sync.dma_start(offs_t[:], offs)
        for s in range(1, PASSES):
            for j in (0, 2):
                nc.sync.dma_start(x_raw[s][:, j:j + 2, :], token_rows(s)[:, j:j + 2, :])
        nc.sync.dma_start(pos_t[0][:], pos1)
        load_scale_rows(w1_sc[0], w1_scales[0:QUAD])
        load_w1_first(0)
        for e in range(QUAD):
            load_w1_rest(e)
        load_scale_rows(w1_sc[1], w1_scales[QUAD:E])
        for e0 in range(QUAD, E, 2):
            load_w1_pair(e0)
        load_scale_rows(w2_sc, w2_scales)
        nc.sync.dma_start(w2_w[:].bitcast(I32), w2_words.rearrange("e s p b -> p (e s) b").bitcast(I32))
        for r, pos in ((3, pos4), (2, pos3), (1, pos2)):
            nc.sync.dma_start(pos_t[r][:], pos)
        for r in (2, 0):
            nc.sync.dma_start(gate_t[:, r:r + 2, :], gate[r:r + 2, 0:P, :].rearrange("r p t -> p r t"))

        x_bf = [keep.tile([P, T, PACK], BF16, name="x_bf%d" % s, align_bytes=64) for s in range(PASSES)]
        x_w12 = keep.tile([P, 2 * T], U32, name="x_w12", align_bytes=64)
        x_w = [x_w0[:, 0:T].bitcast(U32), x_w12[:, 0:T], x_w12[:, T:2 * T]]
        x_sc = [x_sc01[:, 0:T], x_sc01[LIVE:P, 0:T], x_sc2[:]]

        def scalar_copy(dst, src):
            nc.scalar.activation(dst, src, COPY)

        def round_tokens(copy, s, raw, t0):
            dst = x_bf[s][:, t0:t0 + raw.shape[2], :].rearrange("p (c i) j -> p c j i", i=4)
            copy(dst, raw.rearrange("p j (c i) -> p c j i", i=4))

        def quantise_tokens(s, t0, t1):
            nc.vector.quantize_mx(
                out=x_w[s][:, t0:t1].bitcast(FP8X4),
                scales=x_sc[s][:, t0:t1],
                in_=x_bf[s][:, t0:t1, :].rearrange("p t j -> p (t j)"),
            )

        g_w = [keep.tile([P, S], U32, name="g_w%d" % s, align_bytes=64) for s in range(PASSES)]
        g_sc01 = keep.tile([P, S], U8, name="g_sc01", align_bytes=64)
        g_sc = [g_sc01, g_sc1, keep.tile([P, S], U8, name="g_sc2", align_bytes=64)]

        def gather(dst, window, e0, e1):
            entries = offs_t[:, e0 * C // PER_COLUMN:e1 * C // PER_COLUMN]
            nc.vector.tensor_copy(dst[:, e0 * C:e1 * C], window.indirect(entries))

        bank = [psum.tile([P, H], F32, name="bank%d" % e) for e in range(E)]

        def first_product(s, e, start, stop):
            slots = slice(e * C, (e + 1) * C)
            place = (e % QUAD) * PASSES + s
            nc.tensor.matmul_mx(
                out=bank[e][:],
                lhsT=g_w[s][:, slots].bitcast(FP8X4),
                lhsT_scale=g_sc[s][:, slots],
                rhs=w1_w[e, s].bitcast(FP4X4),
                rhs_scale=w1_sc[e // QUAD][:, place * H:(place + 1) * H],
                start=start,
                stop=stop,
            )

        def open_sums(e0, e1):
            for e in range(e0, e1):
                first_product(0, e, True, False)

        def close_sums(e0, order):
            for s in order:
                for e in (e0, e0 + 1):
                    first_product(s, e, False, s == order[-1])

        h_bf = {}

        def hidden(e):
            h_t = ring.tile([P, H], BF16, name="h_t", align_bytes=64)
            nc.scalar.activation(
                h_t[:].rearrange("c (u p d) -> c u p d", u=2, d=2),
                bank[e][:].rearrange("c (p u d) -> c u p d", u=2, d=2),
                SILU,
            )
            pairs = h_t[:].bitcast(F32)
            for u in range(2):
                nc.tensor.transpose(bank[e][:, u * C:(u + 1) * C], pairs[:, u * P:(u + 1) * P], ident[:])
            h_bf[e] = keep.tile([P, C * PACK], BF16, name="h_bf%d" % e, align_bytes=64)
            copy = nc.vector.tensor_copy if 2 <= e < E - 2 else nc.scalar.copy
            copy(
                h_bf[e][:].bitcast(F32).rearrange("p (c u) -> p c u", u=2),
                bank[e][:, 0:2 * C].rearrange("p (u c) -> p c u", u=2),
            )

        h_w = keep.tile([P, S], U32, name="h_w", align_bytes=64)
        h_sc = keep.tile([P, S], U8, name="h_sc", align_bytes=64)

        def quantise_hidden(e):
            slots = slice(e * C, (e + 1) * C)
            nc.vector.quantize_mx(out=h_w[:, slots].bitcast(FP8X4), scales=h_sc[:, slots], in_=h_bf[e][:])

        def second_products(hf, e0, e1, bank_no, copy):
            acc = psum.tile([P, H], F32, name="y%d_%d" % (hf, e0), tag="bank%d" % bank_no)
            for e in range(e0, e1):
                slots = slice(e * C, (e + 1) * C)
                nc.tensor.matmul_mx(
                    out=acc[:, (e - e0) * C:(e - e0 + 1) * C],
                    lhsT=w2_w[:, e, hf * 2 * P:(hf + 1) * 2 * P].bitcast(FP4X4),
                    lhsT_scale=w2_sc[:, e * N + hf * P:e * N + (hf + 1) * P],
                    rhs=h_w[:, slots].bitcast(FP8X4),
                    rhs_scale=h_sc[:, slots],
                    start=True,
                    stop=True,
                )
            copy(y[hf][:, e0 * C:e1 * C], acc[:, 0:(e1 - e0) * C])

        middle = T // 2
        round_tokens(nc.vector.tensor_copy, 0, x_first[0][:], 0)
        quantise_tokens(0, 0, middle)
        round_tokens(nc.vector.tensor_copy, 0, x_first[1][:, :, 0:VECTOR_SHARE_PASS0], middle)
        round_tokens(scalar_copy, 0, x_first[1][:, :, VECTOR_SHARE_PASS0:middle], middle + VECTOR_SHARE_PASS0)
        quantise_tokens(0, middle, T)
        for e0 in range(0, E, QUAD):
            gather(g_w[0], x_w0[:].bitcast(U32), e0, e0 + QUAD)

        split = T - VECTOR_SHARE_PASS1
        round_tokens(scalar_copy, 1, x_raw[1][:, :, 0:split], 0)
        round_tokens(nc.vector.tensor_copy, 1, x_raw[1][:, :, split:T], split)
        quantise_tokens(1, 0, T)
        for e0 in range(0, E, QUAD):
            gather(g_sc01, x_sc01[:], e0, e0 + QUAD)
            cols = slice(e0 * C, (e0 + QUAD) * C)
            nc.gpsimd.dma_start(
                g_sc1[0:SHIFT_ROWS, cols].bitcast(I32), g_sc01[LIVE:LIVE + SHIFT_ROWS, cols].bitcast(I32)
            )
        gather(g_w[1], x_w[1], 0, 2)

        round_tokens(scalar_copy, 2, x_raw[2][:], 0)
        quantise_tokens(2, 0, T)
        for e0, e1 in STEPS:
            if e0 > 0 and e0 % 2 == 0:
                gather(g_w[1], x_w12[:], e0, e0 + 2)
            gather(g_w[2], x_w[2], e0, e1)
            gather(g_sc[2], x_sc2[:], e0, e1)

        for e0 in range(0, E, 2):
            if e0 == 0:
                open_sums(0, QUAD)
            if e0 >= QUAD:
                open_sums(e0, e0 + 2)
            close_sums(e0, (2, 1) if e0 == 0 else (1, 2))
            for e in range(max(e0 - 2, 0), e0):
                hidden(e)
                quantise_hidden(e)
        for e in (E - 2, E - 1):
            hidden(e)
        for e in (E - 2, E - 1):
            quantise_hidden(e)

        second_products(0, 0, QUAD, E - 2, nc.scalar.copy)
        second_products(0, E - 2, E - 1, 0, nc.vector.tensor_copy)
        second_products(0, QUAD, E - 2, E - 1, nc.scalar.copy)
        second_products(0, E - 1, E, 1, nc.vector.tensor_copy)
        second_products(1, 0, QUAD, 1, nc.scalar.copy)
        second_products(1, QUAD, E, E - 1, nc.scalar.copy)

        back = {}
        chunks = T // P
        for hf in range(HALVES):
            sums = [
                psum.tile([P, H], F32, name="sums%d_%d" % (hf, c), tag="bank%d" % SUM_BANKS[hf][c]) for c in range(chunks)
            ]
            for r in range(TOP - 1, 0, -1):
                prod = keep.tile([P, T], F32, name="prod%d_%d" % (hf, r))
                nc.vector.tensor_tensor(prod[:], y[hf][:].indirect(pos_t[r][:]), gate_t[:, r, :], MULT)
                for c in range(chunks):
                    nc.tensor.matmul(
                        sums[c][:, 0:P], prod[:, c * P:(c + 1) * P], ident[:],
                        start=(r == TOP - 1), stop=(r == 1), is_transpose=True,
                    )
            turned = keep.tile([P, T], F32, name="turned%d" % hf)
            for c in range(chunks):
                nc.scalar.copy(turned[:, c * P:(c + 1) * P], sums[c][:, 0:P])
            back[hf] = psum.tile([P, H], F32, name="back%d" % hf, tag="bank%d" % SUM_BANKS[hf][0])
            for c in range(chunks):
                nc.tensor.transpose(back[hf][:, c * P:(c + 1) * P], turned[:, c * P:(c + 1) * P], ident[:])
        for hf, t0, t1 in ((0, 0, T), (1, 0, middle), (1, middle, T)):
            last = keep.tile([P, t1 - t0], F32, name="last%d_%d" % (hf, t0))
            entries = pos_t[0][:, t0 // PER_COLUMN:t1 // PER_COLUMN]
            nc.vector.tensor_tensor(last[:], y[hf][:].indirect(entries), gate_t[:, 0, t0:t1], MULT)
            total = keep.tile([P, t1 - t0], F32, name="total%d_%d" % (hf, t0))
            nc.vector.tensor_tensor(total[:], back[hf][:, t0:t1], last[:], ADD)
            nc.sync.dma_start(out[hf * P:(hf + 1) * P, t0:t1], total[:])
